import numpy as np
import ml_dtypes


def mxq(x, axis, fmt="e4m3"):
    dtype, down = {"e4m3": (ml_dtypes.float8_e4m3fn, 7), "e5m2": (ml_dtypes.float8_e5m2, 14)}[fmt]
    v = np.moveaxis(np.asarray(x, np.float32).astype(ml_dtypes.bfloat16).astype(np.float64), axis, -1)
    blocks = v.reshape(v.shape[:-1] + (-1, 32))
    amax = np.abs(blocks).max(-1, keepdims=True)
    byte = np.maximum(np.where(amax > 0, np.frexp(amax)[1] - 1 + 127, 0) - down, 1)
    scale = np.exp2(byte - 127.0)
    codes = (blocks / scale).astype(np.float32).astype(dtype).astype(np.float64)
    return np.moveaxis((codes * scale).reshape(v.shape), -1, axis)


WIDE = False


def mx_kscale(k):
    if not WIDE:
        return np.ones(k)
    levels = np.array([10, -10, 5, -5, 0])
    if k % 512:
        return np.exp2(np.random.permutation(np.resize(levels, k // 32))).repeat(32)
    a = np.empty((k // 512, 16))
    for p in range(k // 512):
        a[p, :8] = np.random.permutation(np.resize(levels, 8))
        for g in range(8):
            far = levels[np.abs(levels - a[p, g]) >= 10]
            a[p, g + 8] = far[np.random.randint(len(far))]
    return np.exp2(a.ravel()).repeat(32)


def f64(x):
    return np.asarray(x).astype(np.float64)


def striped(idx):
    return np.tile(idx.reshape(-1, 16).T, (8, 1)).astype(np.uint16)


def unstriped(offs):
    return offs[:16].T.reshape(-1).astype(np.int64)


def gelu(v):
    return 0.5 * v * (1.0 + np.tanh(np.sqrt(2.0 / np.pi) * (v + 0.044715 * v**3)))


K, T, D, S, V, N = 512, 4096, 4, 1536, 384, 128


def setup_inputs():
    n = np.random.standard_normal
    s = mx_kscale(K)[:, None]
    return {
        "xT": (n((K, T)) * s).astype(np.float32),
        "w": (n((K, N)) / np.sqrt(K) / s).astype(np.float32),
        "b": (0.3 * n((N, 1))).astype(np.float32),
        "offs": striped(np.random.permutation(T)[:S]),
    }


def reference(xT, w, b, offs):
    idx = unstriped(offs)
    xq = mxq(f64(xT)[:, idx], 0, "e4m3")
    y = mxq(f64(w), 0, "e4m3").T @ xq
    y = gelu(y + f64(b))
    return y.reshape(N, V, D).max(axis=2)

@@ -1,0 +1,126 @@
+from contextlib import ExitStack
+
+import concourse.mybir as mybir
+
+K, T, D, S, V, N = 512, 4096, 4, 1536, 384, 128
+FLOPS = 2 * K * N * S
+
+F32 = mybir.dt.float32
+BF16 = mybir.dt.bfloat16
+U32 = mybir.dt.uint32
+U16 = mybir.dt.uint16
+U8 = mybir.dt.uint8
+FP8X4 = mybir.dt.float8_e4m3fn_x4
+GELU = mybir.ActivationFunctionType.Gelu_apprx_tanh
+MAX = mybir.AluOpType.max
+
+P = 128
+PACK = 4
+STRIPE = 16
+PIECE = 512
+PIECES = S // PIECE
+
+
+def tile_picked_pool_lin_gelu_sub_e_kernel(tc, xT, w, b, offs, out):
+    nc = tc.nc
+    with ExitStack() as ctx:
+        keep = ctx.enter_context(tc.tile_pool(name="keep", bufs=1))
+        psum = ctx.enter_context(tc.psum_pool(name="psum", bufs=1))
+
+        offsets = keep.tile([P, S // STRIPE], U16, name="offsets")
+        rows = [keep.tile([P, T], F32, name=f"rows{j}") for j in range(PACK)]
+        w_raw = keep.tile([P, PACK, N], F32, name="w_raw")
+        bias = keep.tile([P, 1], F32, name="bias")
+
+        x_rows = xT.rearrange("(p j) t -> p j t", j=PACK)
+        nc.sync.dma_start(rows[0][:], x_rows[:, 0, :])
+        nc.sync.dma_start(offsets[:], offs)
+        for j in range(1, PACK):
+            nc.sync.dma_start(rows[j][:], x_rows[:, j, :])
+        nc.sync.dma_start(w_raw[:], w.rearrange("(p j) n -> p j n", j=PACK))
+        nc.sync.dma_start(bias[:], b)
+
+        warm_in = keep.tile([P, 1], F32, name="warm_in")
+        warm_out = keep.tile([P, 1], F32, name="warm_out")
+        nc.vector.memset(warm_in[:], 0.0)
+        nc.scalar.activation(warm_out[:], warm_in[:], GELU)
+
+        grouped = [keep.tile([P, PIECE, PACK], BF16, name=f"grouped{s}", align_bytes=64) for s in range(PIECES)]
+        last = PIECES - 1
+
+        def looked_up(j, s):
+            cols = PIECE // STRIPE
+            return rows[j][:].indirect(offsets[:, s * cols : (s + 1) * cols])
+
+        def interleave(pair, s, u):
+            nc.scalar.copy(grouped[s][:, :, 2 * u : 2 * u + 2], pair[:].rearrange("p e n -> p n e"))
+
+        low = [keep.tile([P, 2, PIECE], F32, name=f"low{s}") for s in range(PIECES)]
+        high = [keep.tile([P, 2, PIECE], F32, name=f"high{s}") for s in range(last)]
+        for s in range(PIECES):
+            nc.vector.tensor_copy(low[s][:, 0, :], looked_up(0, s))
+        for s in range(PIECES):
+            nc.vector.tensor_copy(low[s][:, 1, :], looked_up(1, s))
+            interleave(low[s], s, 0)
+        for s in range(last):
+            nc.vector.tensor_copy(high[s][:, 0, :], looked_up(2, s))
+        nc.vector.tensor_copy(grouped[last][:, :, 2], looked_up(2, last))
+
+        w_grouped = keep.tile([P, N, PACK], BF16, name="w_grouped", align_bytes=64)
+        nc.scalar.copy(w_grouped[:], w_raw[:].rearrange("p j n -> p n j"))
+
+        for s in range(last):
+            nc.vector.tensor_copy(high[s][:, 1, :], looked_up(3, s))
+            interleave(high[s], s, 1)
+        nc.vector.tensor_copy(grouped[last][:, :, 3], looked_up(3, last))
+
+        w_codes = keep.tile([P, N], U32, name="w_codes", align_bytes=64)
+        w_scales = keep.tile([P, N], U8, name="w_scales", align_bytes=64)
+        nc.vector.quantize_mx(
+            out=w_codes[:].bitcast(FP8X4), scales=w_scales[:], in_=w_grouped[:].rearrange("p n j -> p (n j)")
+        )
+
+        spans = [(0, 0, 512), (1, 0, 512), (2, 0, 256), (2, 256, 256)]
+        acts = []
+        for i, (s, start, width) in enumerate(spans):
+            codes = keep.tile([P, width], U32, name=f"codes{i}", align_bytes=64)
+            scales = keep.tile([P, width], U8, name=f"scales{i}", align_bytes=64)
+            nc.vector.quantize_mx(
+                out=codes[:].bitcast(FP8X4),
+                scales=scales[:],
+                in_=grouped[s][:, start : start + width, :].rearrange("p n j -> p (n j)"),
+            )
+            acc = psum.tile([P, width], F32, name=f"acc{i}")
+            nc.tensor.matmul_mx(
+                out=acc[:],
+                lhsT=w_codes[:].bitcast(FP8X4),
+                lhsT_scale=w_scales[:],
+                rhs=codes[:].bitcast(FP8X4),
+                rhs_scale=scales[:],
+                start=True,
+                stop=True,
+            )
+            if s < last:
+                act = keep.tile([P, D, width // D], F32, name=f"act{i}")
+                nc.scalar.activation(act[:], acc[:].rearrange("p (v d) -> p d v", d=D), GELU, bias=bias[:])
+            else:
+                act = keep.tile([P, width // D, D], F32, name=f"act{i}")
+                nc.scalar.activation(act[:], acc[:].rearrange("p (v d) -> p v d", d=D), GELU, bias=bias[:])
+            acts.append(act)
+
+        centres = PIECE // D
+        pooled_a = keep.tile([P, 2 * centres], F32, name="pooled_a")
+        pooled_b = keep.tile([P, centres], F32, name="pooled_b")
+        halves = [keep.tile([P, 2, centres], F32, name=f"half{i}") for i in range(2)]
+        for i in range(2):
+            nc.vector.tensor_tensor(halves[i][:], acts[i][:, 0:2, :], acts[i][:, 2:4, :], MAX)
+        for i in range(2):
+            nc.vector.tensor_tensor(
+                pooled_a[:, i * centres : (i + 1) * centres], halves[i][:, 0, :], halves[i][:, 1, :], MAX
+            )
+        nc.sync.dma_start(out[:, 0 : 2 * centres], pooled_a[:])
+        for i in range(2):
+            nc.vector.tensor_reduce(
+                pooled_b[:, i * 64 : (i + 1) * 64], acts[2 + i][:], mybir.AxisListType.X, MAX
+            )
+        nc.sync.dma_start(out[:, 2 * centres : V], pooled_b[:])

@@ -35,9 +35,9 @@ def tile_picked_pool_lin_gelu_sub_e_kernel(tc, xT, w, b, offs, out):
         x_rows = xT.rearrange("(p j) t -> p j t", j=PACK)
         nc.sync.dma_start(rows[0][:], x_rows[:, 0, :])
         nc.sync.dma_start(offsets[:], offs)
+        nc.sync.dma_start(w_raw[:], w.rearrange("(p j) n -> p j n", j=PACK))
         for j in range(1, PACK):
             nc.sync.dma_start(rows[j][:], x_rows[:, j, :])
-        nc.sync.dma_start(w_raw[:], w.rearrange("(p j) n -> p j n", j=PACK))
         nc.sync.dma_start(bias[:], b)
 
         warm_in = keep.tile([P, 1], F32, name="warm_in")
@@ -59,20 +59,8 @@ def tile_picked_pool_lin_gelu_sub_e_kernel(tc, xT, w, b, offs, out):
         high = [keep.tile([P, 2, PIECE], F32, name=f"high{s}") for s in range(last)]
         for s in range(PIECES):
             nc.vector.tensor_copy(low[s][:, 0, :], looked_up(0, s))
-        for s in range(PIECES):
-            nc.vector.tensor_copy(low[s][:, 1, :], looked_up(1, s))
-            interleave(low[s], s, 0)
-        for s in range(last):
-            nc.vector.tensor_copy(high[s][:, 0, :], looked_up(2, s))
-        nc.vector.tensor_copy(grouped[last][:, :, 2], looked_up(2, last))
-
         w_grouped = keep.tile([P, N, PACK], BF16, name="w_grouped", align_bytes=64)
         nc.scalar.copy(w_grouped[:], w_raw[:].rearrange("p j n -> p n j"))
-
-        for s in range(last):
-            nc.vector.tensor_copy(high[s][:, 1, :], looked_up(3, s))
-            interleave(high[s], s, 1)
-        nc.vector.tensor_copy(grouped[last][:, :, 3], looked_up(3, last))
 
         w_codes = keep.tile([P, N], U32, name="w_codes", align_bytes=64)
         w_scales = keep.tile([P, N], U8, name="w_scales", align_bytes=64)
@@ -80,8 +68,23 @@ def tile_picked_pool_lin_gelu_sub_e_kernel(tc, xT, w, b, offs, out):
             out=w_codes[:].bitcast(FP8X4), scales=w_scales[:], in_=w_grouped[:].rearrange("p n j -> p (n j)")
         )
 
-        spans = [(0, 0, 512), (1, 0, 512), (2, 0, 256), (2, 256, 256)]
-        acts = []
+        for s in range(PIECES):
+            nc.vector.tensor_copy(low[s][:, 1, :], looked_up(1, s))
+            interleave(low[s], s, 0)
+        for s in range(last):
+            nc.vector.tensor_copy(high[s][:, 0, :], looked_up(2, s))
+        nc.vector.tensor_copy(grouped[last][:, :, 2], looked_up(2, last))
+
+        for s in range(last):
+            nc.vector.tensor_copy(high[s][:, 1, :], looked_up(3, s))
+            interleave(high[s], s, 1)
+        nc.vector.tensor_copy(grouped[last][:, :, 3], looked_up(3, last))
+
+        spans = [(0, 0, 256), (0, 256, 256), (2, 0, 256), (2, 256, 256), (1, 0, 256), (1, 256, 128), (1, 384, 128)]
+        centres = PIECE // D
+        acts = {}
+        halves = [keep.tile([P, 2, 2, centres // 2], F32, name=f"half{s}") for s in range(PIECES)]
+        pooled = [keep.tile([P, centres], F32, name=f"pooled{s}") for s in range(PIECES)]
         for i, (s, start, width) in enumerate(spans):
             codes = keep.tile([P, width], U32, name=f"codes{i}", align_bytes=64)
             scales = keep.tile([P, width], U8, name=f"scales{i}", align_bytes=64)
@@ -100,27 +103,43 @@ def tile_picked_pool_lin_gelu_sub_e_kernel(tc, xT, w, b, offs, out):
                 start=True,
                 stop=True,
             )
-            if s < last:
-                act = keep.tile([P, D, width // D], F32, name=f"act{i}")
-                nc.scalar.activation(act[:], acc[:].rearrange("p (v d) -> p d v", d=D), GELU, bias=bias[:])
-            else:
-                act = keep.tile([P, width // D, D], F32, name=f"act{i}")
-                nc.scalar.activation(act[:], acc[:].rearrange("p (v d) -> p v d", d=D), GELU, bias=bias[:])
-            acts.append(act)
+            act = keep.tile([P, D, width // D], F32, name=f"act{i}")
+            nc.scalar.activation(act[:], acc[:].rearrange("p (v d) -> p d v", d=D), GELU, bias=bias[:])
+            acts[(s, start)] = act
 
-        centres = PIECE // D
-        pooled_a = keep.tile([P, 2 * centres], F32, name="pooled_a")
-        pooled_b = keep.tile([P, centres], F32, name="pooled_b")
-        halves = [keep.tile([P, 2, centres], F32, name=f"half{i}") for i in range(2)]
-        for i in range(2):
-            nc.vector.tensor_tensor(halves[i][:], acts[i][:, 0:2, :], acts[i][:, 2:4, :], MAX)
-        for i in range(2):
+        def first_max(s, h):
+            act = acts[(s, h * PIECE // 2)]
+            nc.vector.tensor_tensor(halves[s][:, h, :, :], act[:, 0:2, :], act[:, 2:4, :], MAX)
+
+        def second_max(s, lo, hi):
             nc.vector.tensor_tensor(
-                pooled_a[:, i * centres : (i + 1) * centres], halves[i][:, 0, :], halves[i][:, 1, :], MAX
+                pooled[s][:].rearrange("p (h v) -> p h v", h=2)[:, lo:hi, :],
+                halves[s][:, lo:hi, 0, :],
+                halves[s][:, lo:hi, 1, :],
+                MAX,
             )
-        nc.sync.dma_start(out[:, 0 : 2 * centres], pooled_a[:])
-        for i in range(2):
+
+        def whole_max(s, start, width):
             nc.vector.tensor_reduce(
-                pooled_b[:, i * 64 : (i + 1) * 64], acts[2 + i][:], mybir.AxisListType.X, MAX
+                pooled[s][:, start // D : (start + width) // D],
+                acts[(s, start)][:].rearrange("p d v -> p v d"),
+                mybir.AxisListType.X,
+                MAX,
             )
-        nc.sync.dma_start(out[:, 2 * centres : V], pooled_b[:])
+
+        def store(s):
+            nc.sync.dma_start(out[:, s * centres : (s + 1) * centres], pooled[s][:])
+
+        first_max(0, 0)
+        first_max(0, 1)
+        first_max(2, 0)
+        second_max(0, 0, 2)
+        store(0)
+        first_max(2, 1)
+        first_max(1, 0)
+        second_max(2, 0, 2)
+        store(2)
+        whole_max(1, 256, 128)
+        second_max(1, 0, 1)
+        whole_max(1, 384, 128)
+        store(1)

@@ -35,9 +35,9 @@ def tile_picked_pool_lin_gelu_sub_e_kernel(tc, xT, w, b, offs, out):
         x_rows = xT.rearrange("(p j) t -> p j t", j=PACK)
         nc.sync.dma_start(rows[0][:], x_rows[:, 0, :])
         nc.sync.dma_start(offsets[:], offs)
-        nc.sync.dma_start(w_raw[:], w.rearrange("(p j) n -> p j n", j=PACK))
         for j in range(1, PACK):
             nc.sync.dma_start(rows[j][:], x_rows[:, j, :])
+        nc.sync.dma_start(w_raw[:], w.rearrange("(p j) n -> p j n", j=PACK))
         nc.sync.dma_start(bias[:], b)
 
         warm_in = keep.tile([P, 1], F32, name="warm_in")
@@ -45,8 +45,10 @@ def tile_picked_pool_lin_gelu_sub_e_kernel(tc, xT, w, b, offs, out):
         nc.vector.memset(warm_in[:], 0.0)
         nc.scalar.activation(warm_out[:], warm_in[:], GELU)
 
-        grouped = [keep.tile([P, PIECE, PACK], BF16, name=f"grouped{s}", align_bytes=64) for s in range(PIECES)]
         last = PIECES - 1
+        early = keep.tile([P, last * PIECE, PACK], BF16, name="early", align_bytes=64)
+        late = keep.tile([P, PIECE, PACK], BF16, name="late", align_bytes=64)
+        grouped = [early[:, s * PIECE : (s + 1) * PIECE, :] for s in range(last)] + [late[:]]
 
         def looked_up(j, s):
             cols = PIECE // STRIPE
@@ -59,15 +61,6 @@ def tile_picked_pool_lin_gelu_sub_e_kernel(tc, xT, w, b, offs, out):
         high = [keep.tile([P, 2, PIECE], F32, name=f"high{s}") for s in range(last)]
         for s in range(PIECES):
             nc.vector.tensor_copy(low[s][:, 0, :], looked_up(0, s))
-        w_grouped = keep.tile([P, N, PACK], BF16, name="w_grouped", align_bytes=64)
-        nc.scalar.copy(w_grouped[:], w_raw[:].rearrange("p j n -> p n j"))
-
-        w_codes = keep.tile([P, N], U32, name="w_codes", align_bytes=64)
-        w_scales = keep.tile([P, N], U8, name="w_scales", align_bytes=64)
-        nc.vector.quantize_mx(
-            out=w_codes[:].bitcast(FP8X4), scales=w_scales[:], in_=w_grouped[:].rearrange("p n j -> p (n j)")
-        )
-
         for s in range(PIECES):
             nc.vector.tensor_copy(low[s][:, 1, :], looked_up(1, s))
             interleave(low[s], s, 0)
@@ -75,12 +68,22 @@ def tile_picked_pool_lin_gelu_sub_e_kernel(tc, xT, w, b, offs, out):
             nc.vector.tensor_copy(high[s][:, 0, :], looked_up(2, s))
         nc.vector.tensor_copy(grouped[last][:, :, 2], looked_up(2, last))
 
+        w_grouped = keep.tile([P, N, PACK], BF16, name="w_grouped", align_bytes=64)
+        nc.scalar.copy(w_grouped[:], w_raw[:].rearrange("p j n -> p n j"))
+        nc.scalar.copy(early[:, 0 : last * PIECE : PIECE, 2:4], w_grouped[:, 0:last, 0:2])
+
         for s in range(last):
             nc.vector.tensor_copy(high[s][:, 1, :], looked_up(3, s))
             interleave(high[s], s, 1)
         nc.vector.tensor_copy(grouped[last][:, :, 3], looked_up(3, last))
 
-        spans = [(0, 0, 256), (0, 256, 256), (2, 0, 256), (2, 256, 256), (1, 0, 256), (1, 256, 128), (1, 384, 128)]
+        w_codes = keep.tile([P, N], U32, name="w_codes", align_bytes=64)
+        w_scales = keep.tile([P, N], U8, name="w_scales", align_bytes=64)
+        nc.vector.quantize_mx(
+            out=w_codes[:].bitcast(FP8X4), scales=w_scales[:], in_=w_grouped[:].rearrange("p n j -> p (n j)")
+        )
+
+        spans = [(2, 0, 256), (2, 256, 256), (0, 0, 256), (0, 256, 256), (1, 0, 256), (1, 256, 128), (1, 384, 128)]
         centres = PIECE // D
         acts = {}
         halves = [keep.tile([P, 2, 2, centres // 2], F32, name=f"half{s}") for s in range(PIECES)]
@@ -130,15 +133,15 @@ def tile_picked_pool_lin_gelu_sub_e_kernel(tc, xT, w, b, offs, out):
         def store(s):
             nc.sync.dma_start(out[:, s * centres : (s + 1) * centres], pooled[s][:])
 
-        first_max(0, 0)
-        first_max(0, 1)
         first_max(2, 0)
-        second_max(0, 0, 2)
-        store(0)
         first_max(2, 1)
-        first_max(1, 0)
+        first_max(0, 0)
         second_max(2, 0, 2)
         store(2)
+        first_max(0, 1)
+        first_max(1, 0)
+        second_max(0, 0, 2)
+        store(0)
         whole_max(1, 256, 128)
         second_max(1, 0, 1)
         whole_max(1, 384, 128)

@@ -19,6 +19,13 @@ PACK = 4
 STRIPE = 16
 PIECE = 512
 PIECES = S // PIECE
+CENTRES = PIECE // D
+
+FUSED = PIECES - 1
+
+WIDE, NARROW = PIECE // 2, PIECE // 4
+SPANS = [(s, start, WIDE) for s in (FUSED, 0) for start in (0, WIDE)]
+SPANS = SPANS + [(1, 0, WIDE), (1, WIDE, NARROW), (1, WIDE + NARROW, NARROW)]
 
 
 def tile_picked_pool_lin_gelu_sub_e_kernel(tc, xT, w, b, offs, out):
@@ -45,10 +52,9 @@ def tile_picked_pool_lin_gelu_sub_e_kernel(tc, xT, w, b, offs, out):
         nc.vector.memset(warm_in[:], 0.0)
         nc.scalar.activation(warm_out[:], warm_in[:], GELU)
 
-        last = PIECES - 1
-        early = keep.tile([P, last * PIECE, PACK], BF16, name="early", align_bytes=64)
-        late = keep.tile([P, PIECE, PACK], BF16, name="late", align_bytes=64)
-        grouped = [early[:, s * PIECE : (s + 1) * PIECE, :] for s in range(last)] + [late[:]]
+        staged = keep.tile([P, FUSED * PIECE, PACK], BF16, name="early", align_bytes=64)
+        fused = keep.tile([P, PIECE, PACK], BF16, name="late", align_bytes=64)
+        grouped = [staged[:, s * PIECE : (s + 1) * PIECE, :] for s in range(FUSED)] + [fused[:]]
 
         def looked_up(j, s):
             cols = PIECE // STRIPE
@@ -58,24 +64,24 @@ def tile_picked_pool_lin_gelu_sub_e_kernel(tc, xT, w, b, offs, out):
             nc.scalar.copy(grouped[s][:, :, 2 * u : 2 * u + 2], pair[:].rearrange("p e n -> p n e"))
 
         low = [keep.tile([P, 2, PIECE], F32, name=f"low{s}") for s in range(PIECES)]
-        high = [keep.tile([P, 2, PIECE], F32, name=f"high{s}") for s in range(last)]
+        high = [keep.tile([P, 2, PIECE], F32, name=f"high{s}") for s in range(FUSED)]
         for s in range(PIECES):
             nc.vector.tensor_copy(low[s][:, 0, :], looked_up(0, s))
         for s in range(PIECES):
             nc.vector.tensor_copy(low[s][:, 1, :], looked_up(1, s))
             interleave(low[s], s, 0)
-        for s in range(last):
+        for s in range(FUSED):
             nc.vector.tensor_copy(high[s][:, 0, :], looked_up(2, s))
-        nc.vector.tensor_copy(grouped[last][:, :, 2], looked_up(2, last))
+        nc.vector.tensor_copy(grouped[FUSED][:, :, 2], looked_up(2, FUSED))
 
         w_grouped = keep.tile([P, N, PACK], BF16, name="w_grouped", align_bytes=64)
+        nc.scalar.copy(staged[:, 0 : FUSED * PIECE : PIECE, 2:PACK], w_raw[:, 0:FUSED, 0:2])
         nc.scalar.copy(w_grouped[:], w_raw[:].rearrange("p j n -> p n j"))
-        nc.scalar.copy(early[:, 0 : last * PIECE : PIECE, 2:4], w_grouped[:, 0:last, 0:2])
 
-        for s in range(last):
+        for s in range(FUSED):
             nc.vector.tensor_copy(high[s][:, 1, :], looked_up(3, s))
             interleave(high[s], s, 1)
-        nc.vector.tensor_copy(grouped[last][:, :, 3], looked_up(3, last))
+        nc.vector.tensor_copy(grouped[FUSED][:, :, 3], looked_up(3, FUSED))
 
         w_codes = keep.tile([P, N], U32, name="w_codes", align_bytes=64)
         w_scales = keep.tile([P, N], U8, name="w_scales", align_bytes=64)
@@ -83,12 +89,11 @@ def tile_picked_pool_lin_gelu_sub_e_kernel(tc, xT, w, b, offs, out):
             out=w_codes[:].bitcast(FP8X4), scales=w_scales[:], in_=w_grouped[:].rearrange("p n j -> p (n j)")
         )
 
-        spans = [(2, 0, 256), (2, 256, 256), (0, 0, 256), (0, 256, 256), (1, 0, 256), (1, 256, 128), (1, 384, 128)]
-        centres = PIECE // D
         acts = {}
-        halves = [keep.tile([P, 2, 2, centres // 2], F32, name=f"half{s}") for s in range(PIECES)]
-        pooled = [keep.tile([P, centres], F32, name=f"pooled{s}") for s in range(PIECES)]
-        for i, (s, start, width) in enumerate(spans):
+        halves = [keep.tile([P, 2, 2, CENTRES // 2], F32, name=f"half{s}") for s in range(PIECES)]
+        pooled = [keep.tile([P, CENTRES], F32, name=f"pooled{s}") for s in range(PIECES)]
+
+        for i, (s, start, width) in enumerate(SPANS):
             codes = keep.tile([P, width], U32, name=f"codes{i}", align_bytes=64)
             scales = keep.tile([P, width], U8, name=f"scales{i}", align_bytes=64)
             nc.vector.quantize_mx(
@@ -106,43 +111,48 @@ def tile_picked_pool_lin_gelu_sub_e_kernel(tc, xT, w, b, offs, out):
                 start=True,
                 stop=True,
             )
-            act = keep.tile([P, D, width // D], F32, name=f"act{i}")
-            nc.scalar.activation(act[:], acc[:].rearrange("p (v d) -> p d v", d=D), GELU, bias=bias[:])
+            if width == NARROW:
+                act = keep.tile([P, width // D, D], F32, name=f"act{i}")
+                products = acc[:].rearrange("p (v d) -> p v d", d=D)
+            else:
+                act = keep.tile([P, D, width // D], F32, name=f"act{i}")
+                products = acc[:].rearrange("p (v d) -> p d v", d=D)
+            nc.scalar.activation(act[:], products, GELU, bias=bias[:])
             acts[(s, start)] = act
 
         def first_max(s, h):
-            act = acts[(s, h * PIECE // 2)]
-            nc.vector.tensor_tensor(halves[s][:, h, :, :], act[:, 0:2, :], act[:, 2:4, :], MAX)
+            values = acts[(s, h * WIDE)]
+            nc.vector.tensor_tensor(halves[s][:, h, :, :], values[:, 0:2, :], values[:, 2:D, :], MAX)
 
-        def second_max(s, lo, hi):
+        def second_max(s, count):
             nc.vector.tensor_tensor(
-                pooled[s][:].rearrange("p (h v) -> p h v", h=2)[:, lo:hi, :],
-                halves[s][:, lo:hi, 0, :],
-                halves[s][:, lo:hi, 1, :],
+                pooled[s][:].rearrange("p (h v) -> p h v", h=2)[:, 0:count, :],
+                halves[s][:, 0:count, 0, :],
+                halves[s][:, 0:count, 1, :],
                 MAX,
             )
 
-        def whole_max(s, start, width):
+        def whole_max(s, start):
             nc.vector.tensor_reduce(
-                pooled[s][:, start // D : (start + width) // D],
-                acts[(s, start)][:].rearrange("p d v -> p v d"),
+                pooled[s][:, start // D : (start + NARROW) // D],
+                acts[(s, start)][:],
                 mybir.AxisListType.X,
                 MAX,
             )
 
         def store(s):
-            nc.sync.dma_start(out[:, s * centres : (s + 1) * centres], pooled[s][:])
+            nc.sync.dma_start(out[:, s * CENTRES : (s + 1) * CENTRES], pooled[s][:])
 
-        first_max(2, 0)
-        first_max(2, 1)
+        first_max(FUSED, 0)
+        first_max(FUSED, 1)
         first_max(0, 0)
-        second_max(2, 0, 2)
-        store(2)
+        second_max(FUSED, 2)
+        store(FUSED)
         first_max(0, 1)
         first_max(1, 0)
-        second_max(0, 0, 2)
+        second_max(0, 2)
         store(0)
-        whole_max(1, 256, 128)
-        second_max(1, 0, 1)
-        whole_max(1, 384, 128)
+        whole_max(1, WIDE)
+        second_max(1, 1)
+        whole_max(1, WIDE + NARROW)
         store(1)

from contextlib import ExitStack

import concourse.mybir as mybir

K, T, D, S, V, N = 512, 4096, 4, 1536, 384, 128
FLOPS = 2 * K * N * S

F32 = mybir.dt.float32
BF16 = mybir.dt.bfloat16
U32 = mybir.dt.uint32
U16 = mybir.dt.uint16
U8 = mybir.dt.uint8
FP8X4 = mybir.dt.float8_e4m3fn_x4
GELU = mybir.ActivationFunctionType.Gelu_apprx_tanh
MAX = mybir.AluOpType.max

P = 128
PACK = 4
STRIPE = 16
PIECE = 512
PIECES = S // PIECE
CENTRES = PIECE // D

FUSED = PIECES - 1

WIDE, NARROW = PIECE // 2, PIECE // 4
SPANS = [(s, start, WIDE) for s in (FUSED, 0) for start in (0, WIDE)]
SPANS = SPANS + [(1, 0, WIDE), (1, WIDE, NARROW), (1, WIDE + NARROW, NARROW)]


def tile_picked_pool_lin_gelu_sub_e_kernel(tc, xT, w, b, offs, out):
    nc = tc.nc
    with ExitStack() as ctx:
        keep = ctx.enter_context(tc.tile_pool(name="keep", bufs=1))
        psum = ctx.enter_context(tc.psum_pool(name="psum", bufs=1))

        offsets = keep.tile([P, S // STRIPE], U16, name="offsets")
        rows = [keep.tile([P, T], F32, name=f"rows{j}") for j in range(PACK)]
        w_raw = keep.tile([P, PACK, N], F32, name="w_raw")
        bias = keep.tile([P, 1], F32, name="bias")

        x_rows = xT.rearrange("(p j) t -> p j t", j=PACK)
        nc.sync.dma_start(rows[0][:], x_rows[:, 0, :])
        nc.sync.dma_start(offsets[:], offs)
        for j in range(1, PACK):
            nc.sync.dma_start(rows[j][:], x_rows[:, j, :])
        nc.sync.dma_start(w_raw[:], w.rearrange("(p j) n -> p j n", j=PACK))
        nc.sync.dma_start(bias[:], b)

        warm_in = keep.tile([P, 1], F32, name="warm_in")
        warm_out = keep.tile([P, 1], F32, name="warm_out")
        nc.vector.memset(warm_in[:], 0.0)
        nc.scalar.activation(warm_out[:], warm_in[:], GELU)

        staged = keep.tile([P, FUSED * PIECE, PACK], BF16, name="early", align_bytes=64)
        fused = keep.tile([P, PIECE, PACK], BF16, name="late", align_bytes=64)
        grouped = [staged[:, s * PIECE : (s + 1) * PIECE, :] for s in range(FUSED)] + [fused[:]]

        def looked_up(j, s):
            cols = PIECE // STRIPE
            return rows[j][:].indirect(offsets[:, s * cols : (s + 1) * cols])

        def interleave(pair, s, u):
            nc.scalar.copy(grouped[s][:, :, 2 * u : 2 * u + 2], pair[:].rearrange("p e n -> p n e"))

        low = [keep.tile([P, 2, PIECE], F32, name=f"low{s}") for s in range(PIECES)]
        high = [keep.tile([P, 2, PIECE], F32, name=f"high{s}") for s in range(FUSED)]
        for s in range(PIECES):
            nc.vector.tensor_copy(low[s][:, 0, :], looked_up(0, s))
        for s in range(PIECES):
            nc.vector.tensor_copy(low[s][:, 1, :], looked_up(1, s))
            interleave(low[s], s, 0)
        for s in range(FUSED):
            nc.vector.tensor_copy(high[s][:, 0, :], looked_up(2, s))
        nc.vector.tensor_copy(grouped[FUSED][:, :, 2], looked_up(2, FUSED))

        w_grouped = keep.tile([P, N, PACK], BF16, name="w_grouped", align_bytes=64)
        nc.scalar.copy(staged[:, 0 : FUSED * PIECE : PIECE, 2:PACK], w_raw[:, 0:FUSED, 0:2])
        nc.scalar.copy(w_grouped[:], w_raw[:].rearrange("p j n -> p n j"))

        for s in range(FUSED):
            nc.vector.tensor_copy(high[s][:, 1, :], looked_up(3, s))
            interleave(high[s], s, 1)
        nc.vector.tensor_copy(grouped[FUSED][:, :, 3], looked_up(3, FUSED))

        w_codes = keep.tile([P, N], U32, name="w_codes", align_bytes=64)
        w_scales = keep.tile([P, N], U8, name="w_scales", align_bytes=64)
        nc.vector.quantize_mx(
            out=w_codes[:].bitcast(FP8X4), scales=w_scales[:], in_=w_grouped[:].rearrange("p n j -> p (n j)")
        )

        acts = {}
        halves = [keep.tile([P, 2, 2, CENTRES // 2], F32, name=f"half{s}") for s in range(PIECES)]
        pooled = [keep.tile([P, CENTRES], F32, name=f"pooled{s}") for s in range(PIECES)]

        for i, (s, start, width) in enumerate(SPANS):
            codes = keep.tile([P, width], U32, name=f"codes{i}", align_bytes=64)
            scales = keep.tile([P, width], U8, name=f"scales{i}", align_bytes=64)
            nc.vector.quantize_mx(
                out=codes[:].bitcast(FP8X4),
                scales=scales[:],
                in_=grouped[s][:, start : start + width, :].rearrange("p n j -> p (n j)"),
            )
            acc = psum.tile([P, width], F32, name=f"acc{i}")
            nc.tensor.matmul_mx(
                out=acc[:],
                lhsT=w_codes[:].bitcast(FP8X4),
                lhsT_scale=w_scales[:],
                rhs=codes[:].bitcast(FP8X4),
                rhs_scale=scales[:],
                start=True,
                stop=True,
            )
            if width == NARROW:
                act = keep.tile([P, width // D, D], F32, name=f"act{i}")
                products = acc[:].rearrange("p (v d) -> p v d", d=D)
            else:
                act = keep.tile([P, D, width // D], F32, name=f"act{i}")
                products = acc[:].rearrange("p (v d) -> p d v", d=D)
            nc.scalar.activation(act[:], products, GELU, bias=bias[:])
            acts[(s, start)] = act

        def first_max(s, h):
            values = acts[(s, h * WIDE)]
            nc.vector.tensor_tensor(halves[s][:, h, :, :], values[:, 0:2, :], values[:, 2:D, :], MAX)

        def second_max(s, count):
            nc.vector.tensor_tensor(
                pooled[s][:].rearrange("p (h v) -> p h v", h=2)[:, 0:count, :],
                halves[s][:, 0:count, 0, :],
                halves[s][:, 0:count, 1, :],
                MAX,
            )

        def whole_max(s, start):
            nc.vector.tensor_reduce(
                pooled[s][:, start // D : (start + NARROW) // D],
                acts[(s, start)][:],
                mybir.AxisListType.X,
                MAX,
            )

        def store(s):
            nc.sync.dma_start(out[:, s * CENTRES : (s + 1) * CENTRES], pooled[s][:])

        first_max(FUSED, 0)
        first_max(FUSED, 1)
        first_max(0, 0)
        second_max(FUSED, 2)
        store(FUSED)
        first_max(0, 1)
        first_max(1, 0)
        second_max(0, 2)
        store(0)
        whole_max(1, WIDE)
        second_max(1, 1)
        whole_max(1, WIDE + NARROW)
        store(1)
